import numpy as np
import ml_dtypes


def mxq(x, axis, fmt="e4m3"):
    dtype, down = {"e4m3": (ml_dtypes.float8_e4m3fn, 7), "e5m2": (ml_dtypes.float8_e5m2, 14)}[fmt]
    v = np.moveaxis(np.asarray(x, np.float32).astype(ml_dtypes.bfloat16).astype(np.float64), axis, -1)
    blocks = v.reshape(v.shape[:-1] + (-1, 32))
    amax = np.abs(blocks).max(-1, keepdims=True)
    byte = np.maximum(np.where(amax > 0, np.frexp(amax)[1] - 1 + 127, 0) - down, 1)
    scale = np.exp2(byte - 127.0)
    codes = (blocks / scale).astype(np.float32).astype(dtype).astype(np.float64)
    return np.moveaxis((codes * scale).reshape(v.shape), -1, axis)


WIDE = False


def mx_kscale(k):
    if not WIDE:
        return np.ones(k)
    levels = np.array([10, -10, 5, -5, 0])
    if k % 512:
        return np.exp2(np.random.permutation(np.resize(levels, k // 32))).repeat(32)
    a = np.empty((k // 512, 16))
    for p in range(k // 512):
        a[p, :8] = np.random.permutation(np.resize(levels, 8))
        for g in range(8):
            far = levels[np.abs(levels - a[p, g]) >= 10]
            a[p, g + 8] = far[np.random.randint(len(far))]
    return np.exp2(a.ravel()).repeat(32)


def f64(x):
    return np.asarray(x).astype(np.float64)


def striped8(idx):
    return np.concatenate([x.reshape(-1, 16).T for x in idx]).astype(np.uint16)


def runs(offs, k):
    lists = np.stack([offs[16 * r : 16 * r + 16].T.reshape(-1) for r in range(8)]).astype(np.int64)
    return lists[np.arange(k) % 512 // 64]


def pack_weight(w):
    k, n = w.shape
    w = f64(np.asarray(w, np.float32).astype(ml_dtypes.bfloat16)).reshape(k // 32, 32, n)
    amax = np.abs(w).max(1)
    byte = np.clip(np.where(amax > 0, np.frexp(amax)[1] - 1 + 127 - 7, 1), 1, 254)
    scaled = (w * np.exp2(127.0 - byte)[:, None, :]).reshape(k, n).astype(np.float32)
    words = np.ascontiguousarray(scaled.reshape(k // 512, 128, 4, n).transpose(0, 1, 3, 2)).astype(ml_dtypes.float8_e4m3fn).view(np.uint8)
    return words, np.ascontiguousarray(byte.astype(np.uint8).reshape(k // 512, 16, n))


def unpack_weight(words, scales):
    g, p, n, _ = words.shape
    vals = np.ascontiguousarray(words).view(ml_dtypes.float8_e4m3fn).astype(np.float64) * np.repeat(np.exp2(scales.astype(np.float64) - 127.0), 8, axis=1)[..., None]
    return vals.transpose(0, 1, 3, 2).reshape(g * 512, n)

def planes(y):
    n, m = y.shape
    v = y.astype(np.float32).astype(ml_dtypes.bfloat16).astype(np.float64).reshape(n // 32, 32, m)
    top = np.abs(v).max(1)
    byte = np.clip(np.where(top > 0, np.frexp(top)[1] - 1 + 127 - 7, 1), 1, 254)
    codes = (v * np.exp2(127.0 - byte)[:, None, :]).reshape(n, m).astype(np.float32).astype(ml_dtypes.float8_e4m3fn).view(np.uint8)
    words = codes.reshape(n // 512, 128, 4, m).transpose(0, 1, 3, 2)
    return np.ascontiguousarray(words), np.ascontiguousarray(byte.astype(np.uint8).reshape(n // 512, 16, m))


K, T, S, N, U = 512, 2048, 512, 512, 1024


def setup_inputs():
    n = np.random.standard_normal
    s = mx_kscale(K)[:, None]
    packed_xT = pack_weight(n((K, T)) * s)
    perm = np.stack([np.random.permutation(U) for _ in range(8)])
    return {
        "x_words": packed_xT[0],
        "x_scales": packed_xT[1],
        "w1": (n((K, N)) / np.sqrt(2 * K) / s).astype(np.float32),
        "w2": (n((K, N)) / np.sqrt(2 * K) / s).astype(np.float32),
        "offs": striped8(np.random.randint(0, T, (8, S))),
        "hz": striped8(np.random.randint(0, T, (8, S))),
        "n1": striped8(perm[:, :S]),
        "n2": striped8(perm[:, S:]),
        "n3": striped8(np.stack([np.random.permutation(S) for _ in range(8)])),
    }


def reference(x_words, x_scales, w1, w2, offs, hz, n1, n2, n3):
    xq = unpack_weight(x_words, x_scales)[np.arange(K)[:, None], runs(offs, K)]
    x_hz = unpack_weight(x_words, x_scales)[np.arange(K)[:, None], runs(hz, K)]
    h = mxq(f64(w1), 0, "e4m3").T @ xq + mxq(f64(w2), 0, "e4m3").T @ x_hz
    dn = np.minimum(h, h[np.arange(N)[:, None], runs(n3, N)])
    up = np.maximum(h, h[np.arange(N)[:, None], runs(n3, N)])
    ph = np.zeros((N, U))
    ph[np.arange(N)[:, None], runs(n1, N)] = up
    out = ph.copy()
    out[np.arange(N)[:, None], runs(n2, N)] = dn
    return (out,) + planes(out)

@@ -1,0 +1,165 @@
+from contextlib import ExitStack
+
+import concourse.mybir as mybir
+
+K, T, S, N, U = 512, 2048, 512, 512, 1024
+FLOPS = 2 * 2 * K * N * S
+
+F32 = mybir.dt.float32
+BF16 = mybir.dt.bfloat16
+I32 = mybir.dt.int32
+U32 = mybir.dt.uint32
+U16 = mybir.dt.uint16
+U8 = mybir.dt.uint8
+FP8X4 = mybir.dt.float8_e4m3fn_x4
+COPY = mybir.ActivationFunctionType.Copy
+MAX = mybir.AluOpType.max
+MIN = mybir.AluOpType.min
+
+P = 128
+PACK = 4
+COLS = S // 16
+CHUNK = 256
+ORDER = (0, 2, 3, 1)
+
+
+def tile_picked_ohhpagmx_none_po_kernel(
+    tc, x_words, x_scales, w1, w2, offs, hz, n1, n2, n3, out_0, out_1, out_2
+):
+    nc = tc.nc
+    with ExitStack() as ctx:
+        keep = ctx.enter_context(tc.tile_pool(name="keep", bufs=1))
+        ring = ctx.enter_context(tc.tile_pool(name="ring", bufs=2))
+        psum = ctx.enter_context(tc.psum_pool(name="psum", bufs=1))
+
+        def load_list(name, src):
+            tile = keep.tile([P, COLS], U16, name=name)
+            nc.sync.dma_start(tile[:], src)
+            return tile
+
+        scale_table = keep.tile([P, T], U8, name="scale_table", align_bytes=64)
+        nc.gpsimd.memset(scale_table[:].bitcast(I32), 0)
+        offs_sb = load_list("offs_sb", offs)
+        nc.scalar.dma_start(scale_table[0:P:8, :].bitcast(I32), x_scales[0].bitcast(I32))
+        hz_sb = load_list("hz_sb", hz)
+        word_table = keep.tile([P, T], I32, name="word_table", align_bytes=64)
+        nc.sync.dma_start(word_table[:], x_words[0].rearrange("p c r -> p (c r)").bitcast(I32))
+        w_raw = []
+        for i, w in enumerate((w1, w2)):
+            raw = keep.tile([P, PACK, N], F32, name="w_raw%d" % i)
+            nc.sync.dma_start(raw[:], w.rearrange("(p j) c -> p j c", j=PACK))
+            w_raw.append(raw)
+        n3_sb = load_list("n3_sb", n3)
+
+        x_plane = keep.tile([P, 2 * S], U8, name="x_plane", align_bytes=64)
+        nc.gpsimd.memset(x_plane[:].bitcast(I32), 0)
+
+        picked_scales = keep.tile([P, 2 * S], U8, name="picked_scales", align_bytes=64)
+        for i, lst in enumerate((offs_sb, hz_sb)):
+            nc.vector.tensor_copy(picked_scales[:, i * S : (i + 1) * S], scale_table[:].indirect(lst[:]))
+        for i in range(4):
+            nc.scalar.dma_start(x_plane[i:P:32, :].bitcast(I32), picked_scales[8 * i : P : 32, :].bitcast(I32))
+        n1_sb = load_list("n1_sb", n1)
+        n2_sb = load_list("n2_sb", n2)
+
+        picked_words = []
+        for i, lst in enumerate((offs_sb, hz_sb)):
+            words = keep.tile([P, S], U32, name="picked_words%d" % i, align_bytes=64)
+            nc.vector.tensor_copy(words[:], word_table[:].bitcast(U32).indirect(lst[:]))
+            picked_words.append(words)
+
+        pages = []
+        for t in range(PACK):
+            page = keep.tile([P, U], F32, name="page%d" % t)
+            nc.gpsimd.memset(page[:], 0.0)
+            pages.append(page)
+
+        banks = [psum.tile([P, S], F32, name="bank%d" % t) for t in range(PACK)]
+        for i in range(2):
+            for half in range(2):
+                grouped = keep.tile([P, 2, P, PACK], BF16, name="w_grouped%d_%d" % (i, half), align_bytes=64)
+                src = w_raw[i][:].rearrange("p j (m t) -> p m j t", t=PACK)[:, :, :, 2 * half : 2 * half + 2]
+                dst = grouped[:].rearrange("p t m j -> p m j t")
+                if i == 1 and half == 0:
+                    nc.vector.tensor_copy(dst, src)
+                else:
+                    nc.scalar.activation(dst, src, COPY)
+                codes = keep.tile([P, 2 * P], U32, name="w_codes%d_%d" % (i, half), align_bytes=64)
+                scales = keep.tile([P, 2 * P], U8, name="w_scales%d_%d" % (i, half), align_bytes=64)
+                nc.vector.quantize_mx(
+                    out=codes[:].bitcast(FP8X4), scales=scales[:], in_=grouped[:].rearrange("p t m j -> p (t m j)")
+                )
+                for u in range(2):
+                    nc.tensor.matmul_mx(
+                        out=banks[2 * half + u][:],
+                        lhsT=codes[:, u * P : (u + 1) * P].bitcast(FP8X4),
+                        lhsT_scale=scales[:, u * P : (u + 1) * P],
+                        rhs=picked_words[i][:].bitcast(FP8X4),
+                        rhs_scale=x_plane[:, i * S : (i + 1) * S],
+                        start=(i == 0),
+                        stop=(i == 1),
+                    )
+
+        y_grouped = keep.tile([P, U, PACK], BF16, name="y_grouped", align_bytes=64)
+        out_rows = out_0.rearrange("(p t) c -> t p c", t=PACK)
+
+        def look_up(step):
+            t = ORDER[step]
+            h_t = ring.tile([P, S], F32, name="h")
+            nc.scalar.copy(h_t[:], banks[t][:])
+            g_t = ring.tile([P, S], F32, name="partner")
+            for half in range(2):
+                dst = g_t[:, half * (S // 2) : (half + 1) * (S // 2)]
+                src = h_t[:].indirect(n3_sb[:, half * (COLS // 2) : (half + 1) * (COLS // 2)])
+                if step == 0 and half == 0:
+                    nc.vector.tensor_copy(dst, src)
+                else:
+                    nc.scalar.activation(dst, src, COPY)
+            return h_t, g_t
+
+        def compare(name, pair, op):
+            res = ring.tile([P, S], F32, name=name)
+            nc.vector.tensor_tensor(res[:], pair[0][:], pair[1][:], op)
+            return res
+
+        pair = look_up(0)
+        ahead = look_up(1)
+        up = compare("up", pair, MAX)
+        dn = compare("dn", pair, MIN)
+        for step, t in enumerate(ORDER):
+            more = step + 1 < PACK
+            pair = ahead
+            if step + 2 < PACK:
+                ahead = look_up(step + 2)
+            nc.vector.tensor_copy(pages[t][:].indirect(n1_sb[:]), up[:])
+            if more:
+                up = compare("up", pair, MAX)
+            nc.vector.tensor_copy(pages[t][:].indirect(n2_sb[:]), dn[:])
+            if more:
+                dn = compare("dn", pair, MIN)
+            nc.sync.dma_start(out_rows[t], pages[t][:])
+            if more:
+                nc.scalar.copy(y_grouped[:, :, t], pages[t][:])
+
+        last = ORDER[-1]
+        y_codes = keep.tile([P, U], I32, name="y_codes", align_bytes=64)
+        y_scales = keep.tile([P, U], U8, name="y_scales", align_bytes=64)
+        chunks = [slice(c, c + CHUNK) for c in range(0, U, CHUNK)]
+        for cols in chunks[:2]:
+            nc.vector.tensor_copy(y_grouped[:, cols, last], pages[last][:, cols])
+        for cols in chunks[2:]:
+            nc.scalar.copy(y_grouped[:, cols, last], pages[last][:, cols])
+        out_words = out_1[0].rearrange("p c r -> p (c r)").bitcast(I32)
+        for c, cols in enumerate(chunks):
+            nc.vector.quantize_mx(
+                out=y_codes[:, cols].bitcast(FP8X4),
+                scales=y_scales[:, cols],
+                in_=y_grouped[:, cols, :].rearrange("p c t -> p (c t)"),
+            )
+            if c % 2 == 1:
+                both = slice(cols.stop - 2 * CHUNK, cols.stop)
+                nc.sync.dma_start(out_words[:, both], y_codes[:, both])
+        out_scales = out_2[0].bitcast(I32)
+        for q in range(4):
+            queue = nc.sync if q < 2 else nc.scalar
+            queue.dma_start(out_scales[4 * q : 4 * q + 4, :], y_scales[32 * q : 32 * q + 4, :].bitcast(I32))

@@ -38,29 +38,28 @@ def tile_picked_ohhpagmx_none_po_kernel(
             return tile
 
         scale_table = keep.tile([P, T], U8, name="scale_table", align_bytes=64)
-        nc.gpsimd.memset(scale_table[:].bitcast(I32), 0)
+        nc.vector.memset(scale_table[:].bitcast(I32), 0)
+        x_plane = keep.tile([P, 2 * S], U8, name="x_plane", align_bytes=64)
+        nc.vector.memset(x_plane[:].bitcast(I32), 0)
         offs_sb = load_list("offs_sb", offs)
-        nc.scalar.dma_start(scale_table[0:P:8, :].bitcast(I32), x_scales[0].bitcast(I32))
-        hz_sb = load_list("hz_sb", hz)
         word_table = keep.tile([P, T], I32, name="word_table", align_bytes=64)
-        nc.sync.dma_start(word_table[:], x_words[0].rearrange("p c r -> p (c r)").bitcast(I32))
+        nc.scalar.dma_start(word_table[:], x_words[0].rearrange("p c r -> p (c r)").bitcast(I32))
+        hz_sb = load_list("hz_sb", hz)
+        nc.sync.dma_start(scale_table[0:P:8, :].bitcast(I32), x_scales[0].bitcast(I32))
         w_raw = []
         for i, w in enumerate((w1, w2)):
             raw = keep.tile([P, PACK, N], F32, name="w_raw%d" % i)
-            nc.sync.dma_start(raw[:], w.rearrange("(p j) c -> p j c", j=PACK))
+            nc.scalar.dma_start(raw[:], w.rearrange("(p j) c -> p j c", j=PACK))
             w_raw.append(raw)
         n3_sb = load_list("n3_sb", n3)
-
-        x_plane = keep.tile([P, 2 * S], U8, name="x_plane", align_bytes=64)
-        nc.gpsimd.memset(x_plane[:].bitcast(I32), 0)
+        n1_sb = load_list("n1_sb", n1)
+        n2_sb = load_list("n2_sb", n2)
 
         picked_scales = keep.tile([P, 2 * S], U8, name="picked_scales", align_bytes=64)
         for i, lst in enumerate((offs_sb, hz_sb)):
             nc.vector.tensor_copy(picked_scales[:, i * S : (i + 1) * S], scale_table[:].indirect(lst[:]))
         for i in range(4):
-            nc.scalar.dma_start(x_plane[i:P:32, :].bitcast(I32), picked_scales[8 * i : P : 32, :].bitcast(I32))
-        n1_sb = load_list("n1_sb", n1)
-        n2_sb = load_list("n2_sb", n2)
+            nc.sync.dma_start(x_plane[i:P:32, :].bitcast(I32), picked_scales[8 * i : P : 32, :].bitcast(I32))
 
         picked_words = []
         for i, lst in enumerate((offs_sb, hz_sb)):
@@ -74,9 +73,9 @@ def tile_picked_ohhpagmx_none_po_kernel(
             nc.gpsimd.memset(page[:], 0.0)
             pages.append(page)
 
-        banks = [psum.tile([P, S], F32, name="bank%d" % t) for t in range(PACK)]
-        for i in range(2):
-            for half in range(2):
+        w_codes, w_scales = {}, {}
+        for half in range(2):
+            for i in range(2):
                 grouped = keep.tile([P, 2, P, PACK], BF16, name="w_grouped%d_%d" % (i, half), align_bytes=64)
                 src = w_raw[i][:].rearrange("p j (m t) -> p m j t", t=PACK)[:, :, :, 2 * half : 2 * half + 2]
                 dst = grouped[:].rearrange("p t m j -> p m j t")
@@ -90,53 +89,75 @@ def tile_picked_ohhpagmx_none_po_kernel(
                     out=codes[:].bitcast(FP8X4), scales=scales[:], in_=grouped[:].rearrange("p t m j -> p (t m j)")
                 )
                 for u in range(2):
-                    nc.tensor.matmul_mx(
-                        out=banks[2 * half + u][:],
-                        lhsT=codes[:, u * P : (u + 1) * P].bitcast(FP8X4),
-                        lhsT_scale=scales[:, u * P : (u + 1) * P],
-                        rhs=picked_words[i][:].bitcast(FP8X4),
-                        rhs_scale=x_plane[:, i * S : (i + 1) * S],
-                        start=(i == 0),
-                        stop=(i == 1),
-                    )
+                    w_codes[i, 2 * half + u] = codes[:, u * P : (u + 1) * P]
+                    w_scales[i, 2 * half + u] = scales[:, u * P : (u + 1) * P]
+
+        def product(name, t, lo, hi):
+            bank = psum.tile([P, hi - lo], F32, name=name)
+            for i in range(2):
+                nc.tensor.matmul_mx(
+                    out=bank[:],
+                    lhsT=w_codes[i, t].bitcast(FP8X4),
+                    lhsT_scale=w_scales[i, t],
+                    rhs=picked_words[i][:, lo:hi].bitcast(FP8X4),
+                    rhs_scale=x_plane[:, i * S + lo : i * S + hi],
+                    start=(i == 0),
+                    stop=(i == 1),
+                )
+            return bank
+
+        first_banks = [product("first_bank%d" % u, ORDER[0], u * (S // 2), (u + 1) * (S // 2)) for u in range(2)]
+        banks = {t: product("bank%d" % t, t, 0, S) for t in ORDER[1:]}
 
         y_grouped = keep.tile([P, U, PACK], BF16, name="y_grouped", align_bytes=64)
         out_rows = out_0.rearrange("(p t) c -> t p c", t=PACK)
 
+        def entries(lst, lo, hi):
+            return lst[:, lo // 16 : hi // 16]
+
         def look_up(step):
-            t = ORDER[step]
             h_t = ring.tile([P, S], F32, name="h")
-            nc.scalar.copy(h_t[:], banks[t][:])
+            if step == 0:
+                nc.vector.tensor_copy(h_t[:, : S // 2], first_banks[0][:])
+                nc.scalar.copy(h_t[:, S // 2 :], first_banks[1][:])
+                cuts = (0, S // 4, S // 2, S)
+            else:
+                nc.scalar.copy(h_t[:], banks[ORDER[step]][:])
+                cuts = (0, S // 2, S)
             g_t = ring.tile([P, S], F32, name="partner")
-            for half in range(2):
-                dst = g_t[:, half * (S // 2) : (half + 1) * (S // 2)]
-                src = h_t[:].indirect(n3_sb[:, half * (COLS // 2) : (half + 1) * (COLS // 2)])
-                if step == 0 and half == 0:
-                    nc.vector.tensor_copy(dst, src)
-                else:
-                    nc.scalar.activation(dst, src, COPY)
+            for lo, hi in zip(cuts, cuts[1:]):
+                nc.scalar.activation(g_t[:, lo:hi], h_t[:].indirect(entries(n3_sb, lo, hi)), COPY)
             return h_t, g_t
 
-        def compare(name, pair, op):
-            res = ring.tile([P, S], F32, name=name)
-            nc.vector.tensor_tensor(res[:], pair[0][:], pair[1][:], op)
-            return res
+        def compare(res, pair, op, lo=0, hi=S):
+            nc.vector.tensor_tensor(res[:, lo:hi], pair[0][:, lo:hi], pair[1][:, lo:hi], op)
+
+        def put(t, lst, values, lo=0, hi=S):
+            nc.vector.tensor_copy(pages[t][:].indirect(entries(lst, lo, hi)), values[:, lo:hi])
 
         pair = look_up(0)
         ahead = look_up(1)
-        up = compare("up", pair, MAX)
-        dn = compare("dn", pair, MIN)
+        up = ring.tile([P, S], F32, name="up")
+        dn = ring.tile([P, S], F32, name="dn")
+        head = S // 4
+        compare(up, pair, MAX, 0, head)
+        compare(dn, pair, MIN, 0, head)
+        put(ORDER[0], n1_sb, up, 0, head)
+        compare(up, pair, MAX, head, S)
+        compare(dn, pair, MIN, head, S)
         for step, t in enumerate(ORDER):
             more = step + 1 < PACK
             pair = ahead
             if step + 2 < PACK:
                 ahead = look_up(step + 2)
-            nc.vector.tensor_copy(pages[t][:].indirect(n1_sb[:]), up[:])
+            put(t, n1_sb, up, head if step == 0 else 0, S)
             if more:
-                up = compare("up", pair, MAX)
-            nc.vector.tensor_copy(pages[t][:].indirect(n2_sb[:]), dn[:])
+                up = ring.tile([P, S], F32, name="up")
+                compare(up, pair, MAX)
+            put(t, n2_sb, dn)
             if more:
-                dn = compare("dn", pair, MIN)
+                dn = ring.tile([P, S], F32, name="dn")
+                compare(dn, pair, MIN)
             nc.sync.dma_start(out_rows[t], pages[t][:])
             if more:
                 nc.scalar.copy(y_grouped[:, :, t], pages[t][:])
@@ -156,9 +177,9 @@ def tile_picked_ohhpagmx_none_po_kernel(
                 scales=y_scales[:, cols],
                 in_=y_grouped[:, cols, :].rearrange("p c t -> p (c t)"),
             )
-            if c % 2 == 1:
-                both = slice(cols.stop - 2 * CHUNK, cols.stop)
-                nc.sync.dma_start(out_words[:, both], y_codes[:, both])
+            if c >= 1:
+                done = slice(0 if c == 1 else cols.start, cols.stop)
+                nc.sync.dma_start(out_words[:, done], y_codes[:, done])
         out_scales = out_2[0].bitcast(I32)
         for q in range(4):
             queue = nc.sync if q < 2 else nc.scalar

@@ -21,6 +21,7 @@ PACK = 4
 COLS = S // 16
 CHUNK = 256
 ORDER = (0, 2, 3, 1)
+VECTOR_TILES = (1, 1)
 
 
 def tile_picked_ohhpagmx_none_po_kernel(
@@ -30,31 +31,33 @@ def tile_picked_ohhpagmx_none_po_kernel(
     with ExitStack() as ctx:
         keep = ctx.enter_context(tc.tile_pool(name="keep", bufs=1))
         ring = ctx.enter_context(tc.tile_pool(name="ring", bufs=2))
-        psum = ctx.enter_context(tc.psum_pool(name="psum", bufs=1))
+        psum = ctx.enter_context(tc.psum_pool(name="psum", bufs=2))
 
         def load_list(name, src):
             tile = keep.tile([P, COLS], U16, name=name)
             nc.sync.dma_start(tile[:], src)
             return tile
 
-        scale_table = keep.tile([P, T], U8, name="scale_table", align_bytes=64)
+        scale_table = keep.tile([P, T], U8, name="scale_table", tag="shared", align_bytes=64)
         nc.vector.memset(scale_table[:].bitcast(I32), 0)
-        x_plane = keep.tile([P, 2 * S], U8, name="x_plane", align_bytes=64)
-        nc.vector.memset(x_plane[:].bitcast(I32), 0)
         offs_sb = load_list("offs_sb", offs)
-        word_table = keep.tile([P, T], I32, name="word_table", align_bytes=64)
-        nc.scalar.dma_start(word_table[:], x_words[0].rearrange("p c r -> p (c r)").bitcast(I32))
         hz_sb = load_list("hz_sb", hz)
+        n3_sb = load_list("n3_sb", n3)
+        word_table = keep.tile([P, T], I32, name="word_table", align_bytes=64)
+        words_in = x_words[0].rearrange("p c r -> p (c r)").bitcast(I32)
+        nc.sync.dma_start(word_table[:, : T // 4], words_in[:, : T // 4])
         nc.sync.dma_start(scale_table[0:P:8, :].bitcast(I32), x_scales[0].bitcast(I32))
+        nc.sync.dma_start(word_table[:, T // 4 :], words_in[:, T // 4 :])
         w_raw = []
         for i, w in enumerate((w1, w2)):
             raw = keep.tile([P, PACK, N], F32, name="w_raw%d" % i)
-            nc.scalar.dma_start(raw[:], w.rearrange("(p j) c -> p j c", j=PACK))
+            nc.sync.dma_start(raw[:], w.rearrange("(p j) c -> p j c", j=PACK))
             w_raw.append(raw)
-        n3_sb = load_list("n3_sb", n3)
         n1_sb = load_list("n1_sb", n1)
         n2_sb = load_list("n2_sb", n2)
 
+        x_plane = keep.tile([P, 2 * S], U8, name="x_plane", align_bytes=64)
+        nc.vector.memset(x_plane[:].bitcast(I32), 0)
         picked_scales = keep.tile([P, 2 * S], U8, name="picked_scales", align_bytes=64)
         for i, lst in enumerate((offs_sb, hz_sb)):
             nc.vector.tensor_copy(picked_scales[:, i * S : (i + 1) * S], scale_table[:].indirect(lst[:]))
@@ -63,37 +66,44 @@ def tile_picked_ohhpagmx_none_po_kernel(
 
         picked_words = []
         for i, lst in enumerate((offs_sb, hz_sb)):
-            words = keep.tile([P, S], U32, name="picked_words%d" % i, align_bytes=64)
+            words = keep.tile([P, S], U32, name="picked_words%d" % i, tag=("shared", "words_hz")[i], align_bytes=64)
             nc.vector.tensor_copy(words[:], word_table[:].bitcast(U32).indirect(lst[:]))
             picked_words.append(words)
 
         pages = []
         for t in range(PACK):
             page = keep.tile([P, U], F32, name="page%d" % t)
-            nc.gpsimd.memset(page[:], 0.0)
+            if t == 0:
+                nc.vector.memset(page[:], 0.0)
+            else:
+                nc.scalar.activation(page[:], pages[0][:], COPY)
             pages.append(page)
 
         w_codes, w_scales = {}, {}
-        for half in range(2):
-            for i in range(2):
-                grouped = keep.tile([P, 2, P, PACK], BF16, name="w_grouped%d_%d" % (i, half), align_bytes=64)
-                src = w_raw[i][:].rearrange("p j (m t) -> p m j t", t=PACK)[:, :, :, 2 * half : 2 * half + 2]
+        for i, split in enumerate(VECTOR_TILES):
+            for lo, hi in ((0, split), (split, PACK)):
+                tag = "%d_%d" % (i, lo)
+                grouped = keep.tile([P, hi - lo, P, PACK], BF16, name="w_grouped" + tag, align_bytes=64)
+                src = w_raw[i][:].rearrange("p j (m t) -> p m j t", t=PACK)[:, :, :, lo:hi]
                 dst = grouped[:].rearrange("p t m j -> p m j t")
-                if i == 1 and half == 0:
+                if i == 1 and lo == 0:
+                    nc.vector.tensor_copy(dst[:, : P // 2], src[:, : P // 2])
+                    nc.scalar.activation(dst[:, P // 2 :], src[:, P // 2 :], COPY)
+                elif i == 1 or lo == 0:
                     nc.vector.tensor_copy(dst, src)
                 else:
                     nc.scalar.activation(dst, src, COPY)
-                codes = keep.tile([P, 2 * P], U32, name="w_codes%d_%d" % (i, half), align_bytes=64)
-                scales = keep.tile([P, 2 * P], U8, name="w_scales%d_%d" % (i, half), align_bytes=64)
+                codes = keep.tile([P, (hi - lo) * P], U32, name="w_codes" + tag, align_bytes=64)
+                scales = keep.tile([P, (hi - lo) * P], U8, name="w_scales" + tag, align_bytes=64)
                 nc.vector.quantize_mx(
                     out=codes[:].bitcast(FP8X4), scales=scales[:], in_=grouped[:].rearrange("p t m j -> p (t m j)")
                 )
-                for u in range(2):
-                    w_codes[i, 2 * half + u] = codes[:, u * P : (u + 1) * P]
-                    w_scales[i, 2 * half + u] = scales[:, u * P : (u + 1) * P]
+                for t in range(lo, hi):
+                    w_codes[i, t] = codes[:, (t - lo) * P : (t - lo + 1) * P]
+                    w_scales[i, t] = scales[:, (t - lo) * P : (t - lo + 1) * P]
 
         def product(name, t, lo, hi):
-            bank = psum.tile([P, hi - lo], F32, name=name)
+            bank = psum.tile([P, hi - lo], F32, name=name, tag="bank")
             for i in range(2):
                 nc.tensor.matmul_mx(
                     out=bank[:],
@@ -107,7 +117,6 @@ def tile_picked_ohhpagmx_none_po_kernel(
             return bank
 
         first_banks = [product("first_bank%d" % u, ORDER[0], u * (S // 2), (u + 1) * (S // 2)) for u in range(2)]
-        banks = {t: product("bank%d" % t, t, 0, S) for t in ORDER[1:]}
 
         y_grouped = keep.tile([P, U, PACK], BF16, name="y_grouped", align_bytes=64)
         out_rows = out_0.rearrange("(p t) c -> t p c", t=PACK)
@@ -115,14 +124,15 @@ def tile_picked_ohhpagmx_none_po_kernel(
         def entries(lst, lo, hi):
             return lst[:, lo // 16 : hi // 16]
 
+
         def look_up(step):
             h_t = ring.tile([P, S], F32, name="h")
             if step == 0:
-                nc.vector.tensor_copy(h_t[:, : S // 2], first_banks[0][:])
+                nc.scalar.copy(h_t[:, : S // 2], first_banks[0][:])
                 nc.scalar.copy(h_t[:, S // 2 :], first_banks[1][:])
                 cuts = (0, S // 4, S // 2, S)
             else:
-                nc.scalar.copy(h_t[:], banks[ORDER[step]][:])
+                nc.scalar.copy(h_t[:], product("bank", ORDER[step], 0, S)[:])
                 cuts = (0, S // 2, S)
             g_t = ring.tile([P, S], F32, name="partner")
             for lo, hi in zip(cuts, cuts[1:]):

@@ -83,7 +83,7 @@ def tile_picked_ohhpagmx_none_po_kernel(
         for i, split in enumerate(VECTOR_TILES):
             for lo, hi in ((0, split), (split, PACK)):
                 tag = "%d_%d" % (i, lo)
-                grouped = keep.tile([P, hi - lo, P, PACK], BF16, name="w_grouped" + tag, align_bytes=64)
+                grouped = keep.tile([P, hi - lo, P, PACK], BF16, name="w_grouped" + tag, tag=("w1_grouped" + tag, "w2_grouped")[i], align_bytes=64)
                 src = w_raw[i][:].rearrange("p j (m t) -> p m j t", t=PACK)[:, :, :, lo:hi]
                 dst = grouped[:].rearrange("p t m j -> p m j t")
                 if i == 1 and lo == 0:

from contextlib import ExitStack

import concourse.mybir as mybir

K, T, S, N, U = 512, 2048, 512, 512, 1024
FLOPS = 2 * 2 * K * N * S

F32 = mybir.dt.float32
BF16 = mybir.dt.bfloat16
I32 = mybir.dt.int32
U32 = mybir.dt.uint32
U16 = mybir.dt.uint16
U8 = mybir.dt.uint8
FP8X4 = mybir.dt.float8_e4m3fn_x4
COPY = mybir.ActivationFunctionType.Copy
MAX = mybir.AluOpType.max
MIN = mybir.AluOpType.min

P = 128
PACK = 4
COLS = S // 16
CHUNK = 256
ORDER = (0, 2, 3, 1)
VECTOR_TILES = (1, 1)


def tile_picked_ohhpagmx_none_po_kernel(
    tc, x_words, x_scales, w1, w2, offs, hz, n1, n2, n3, out_0, out_1, out_2
):
    nc = tc.nc
    with ExitStack() as ctx:
        keep = ctx.enter_context(tc.tile_pool(name="keep", bufs=1))
        ring = ctx.enter_context(tc.tile_pool(name="ring", bufs=2))
        psum = ctx.enter_context(tc.psum_pool(name="psum", bufs=2))

        def load_list(name, src):
            tile = keep.tile([P, COLS], U16, name=name)
            nc.sync.dma_start(tile[:], src)
            return tile

        scale_table = keep.tile([P, T], U8, name="scale_table", tag="shared", align_bytes=64)
        nc.vector.memset(scale_table[:].bitcast(I32), 0)
        offs_sb = load_list("offs_sb", offs)
        hz_sb = load_list("hz_sb", hz)
        n3_sb = load_list("n3_sb", n3)
        word_table = keep.tile([P, T], I32, name="word_table", align_bytes=64)
        words_in = x_words[0].rearrange("p c r -> p (c r)").bitcast(I32)
        nc.sync.dma_start(word_table[:, : T // 4], words_in[:, : T // 4])
        nc.sync.dma_start(scale_table[0:P:8, :].bitcast(I32), x_scales[0].bitcast(I32))
        nc.sync.dma_start(word_table[:, T // 4 :], words_in[:, T // 4 :])
        w_raw = []
        for i, w in enumerate((w1, w2)):
            raw = keep.tile([P, PACK, N], F32, name="w_raw%d" % i)
            nc.sync.dma_start(raw[:], w.rearrange("(p j) c -> p j c", j=PACK))
            w_raw.append(raw)
        n1_sb = load_list("n1_sb", n1)
        n2_sb = load_list("n2_sb", n2)

        x_plane = keep.tile([P, 2 * S], U8, name="x_plane", align_bytes=64)
        nc.vector.memset(x_plane[:].bitcast(I32), 0)
        picked_scales = keep.tile([P, 2 * S], U8, name="picked_scales", align_bytes=64)
        for i, lst in enumerate((offs_sb, hz_sb)):
            nc.vector.tensor_copy(picked_scales[:, i * S : (i + 1) * S], scale_table[:].indirect(lst[:]))
        for i in range(4):
            nc.sync.dma_start(x_plane[i:P:32, :].bitcast(I32), picked_scales[8 * i : P : 32, :].bitcast(I32))

        picked_words = []
        for i, lst in enumerate((offs_sb, hz_sb)):
            words = keep.tile([P, S], U32, name="picked_words%d" % i, tag=("shared", "words_hz")[i], align_bytes=64)
            nc.vector.tensor_copy(words[:], word_table[:].bitcast(U32).indirect(lst[:]))
            picked_words.append(words)

        pages = []
        for t in range(PACK):
            page = keep.tile([P, U], F32, name="page%d" % t)
            if t == 0:
                nc.vector.memset(page[:], 0.0)
            else:
                nc.scalar.activation(page[:], pages[0][:], COPY)
            pages.append(page)

        w_codes, w_scales = {}, {}
        for i, split in enumerate(VECTOR_TILES):
            for lo, hi in ((0, split), (split, PACK)):
                tag = "%d_%d" % (i, lo)
                grouped = keep.tile([P, hi - lo, P, PACK], BF16, name="w_grouped" + tag, tag=("w1_grouped" + tag, "w2_grouped")[i], align_bytes=64)
                src = w_raw[i][:].rearrange("p j (m t) -> p m j t", t=PACK)[:, :, :, lo:hi]
                dst = grouped[:].rearrange("p t m j -> p m j t")
                if i == 1 and lo == 0:
                    nc.vector.tensor_copy(dst[:, : P // 2], src[:, : P // 2])
                    nc.scalar.activation(dst[:, P // 2 :], src[:, P // 2 :], COPY)
                elif i == 1 or lo == 0:
                    nc.vector.tensor_copy(dst, src)
                else:
                    nc.scalar.activation(dst, src, COPY)
                codes = keep.tile([P, (hi - lo) * P], U32, name="w_codes" + tag, align_bytes=64)
                scales = keep.tile([P, (hi - lo) * P], U8, name="w_scales" + tag, align_bytes=64)
                nc.vector.quantize_mx(
                    out=codes[:].bitcast(FP8X4), scales=scales[:], in_=grouped[:].rearrange("p t m j -> p (t m j)")
                )
                for t in range(lo, hi):
                    w_codes[i, t] = codes[:, (t - lo) * P : (t - lo + 1) * P]
                    w_scales[i, t] = scales[:, (t - lo) * P : (t - lo + 1) * P]

        def product(name, t, lo, hi):
            bank = psum.tile([P, hi - lo], F32, name=name, tag="bank")
            for i in range(2):
                nc.tensor.matmul_mx(
                    out=bank[:],
                    lhsT=w_codes[i, t].bitcast(FP8X4),
                    lhsT_scale=w_scales[i, t],
                    rhs=picked_words[i][:, lo:hi].bitcast(FP8X4),
                    rhs_scale=x_plane[:, i * S + lo : i * S + hi],
                    start=(i == 0),
                    stop=(i == 1),
                )
            return bank

        first_banks = [product("first_bank%d" % u, ORDER[0], u * (S // 2), (u + 1) * (S // 2)) for u in range(2)]

        y_grouped = keep.tile([P, U, PACK], BF16, name="y_grouped", align_bytes=64)
        out_rows = out_0.rearrange("(p t) c -> t p c", t=PACK)

        def entries(lst, lo, hi):
            return lst[:, lo // 16 : hi // 16]


        def look_up(step):
            h_t = ring.tile([P, S], F32, name="h")
            if step == 0:
                nc.scalar.copy(h_t[:, : S // 2], first_banks[0][:])
                nc.scalar.copy(h_t[:, S // 2 :], first_banks[1][:])
                cuts = (0, S // 4, S // 2, S)
            else:
                nc.scalar.copy(h_t[:], product("bank", ORDER[step], 0, S)[:])
                cuts = (0, S // 2, S)
            g_t = ring.tile([P, S], F32, name="partner")
            for lo, hi in zip(cuts, cuts[1:]):
                nc.scalar.activation(g_t[:, lo:hi], h_t[:].indirect(entries(n3_sb, lo, hi)), COPY)
            return h_t, g_t

        def compare(res, pair, op, lo=0, hi=S):
            nc.vector.tensor_tensor(res[:, lo:hi], pair[0][:, lo:hi], pair[1][:, lo:hi], op)

        def put(t, lst, values, lo=0, hi=S):
            nc.vector.tensor_copy(pages[t][:].indirect(entries(lst, lo, hi)), values[:, lo:hi])

        pair = look_up(0)
        ahead = look_up(1)
        up = ring.tile([P, S], F32, name="up")
        dn = ring.tile([P, S], F32, name="dn")
        head = S // 4
        compare(up, pair, MAX, 0, head)
        compare(dn, pair, MIN, 0, head)
        put(ORDER[0], n1_sb, up, 0, head)
        compare(up, pair, MAX, head, S)
        compare(dn, pair, MIN, head, S)
        for step, t in enumerate(ORDER):
            more = step + 1 < PACK
            pair = ahead
            if step + 2 < PACK:
                ahead = look_up(step + 2)
            put(t, n1_sb, up, head if step == 0 else 0, S)
            if more:
                up = ring.tile([P, S], F32, name="up")
                compare(up, pair, MAX)
            put(t, n2_sb, dn)
            if more:
                dn = ring.tile([P, S], F32, name="dn")
                compare(dn, pair, MIN)
            nc.sync.dma_start(out_rows[t], pages[t][:])
            if more:
                nc.scalar.copy(y_grouped[:, :, t], pages[t][:])

        last = ORDER[-1]
        y_codes = keep.tile([P, U], I32, name="y_codes", align_bytes=64)
        y_scales = keep.tile([P, U], U8, name="y_scales", align_bytes=64)
        chunks = [slice(c, c + CHUNK) for c in range(0, U, CHUNK)]
        for cols in chunks[:2]:
            nc.vector.tensor_copy(y_grouped[:, cols, last], pages[last][:, cols])
        for cols in chunks[2:]:
            nc.scalar.copy(y_grouped[:, cols, last], pages[last][:, cols])
        out_words = out_1[0].rearrange("p c r -> p (c r)").bitcast(I32)
        for c, cols in enumerate(chunks):
            nc.vector.quantize_mx(
                out=y_codes[:, cols].bitcast(FP8X4),
                scales=y_scales[:, cols],
                in_=y_grouped[:, cols, :].rearrange("p c t -> p (c t)"),
            )
            if c >= 1:
                done = slice(0 if c == 1 else cols.start, cols.stop)
                nc.sync.dma_start(out_words[:, done], y_codes[:, done])
        out_scales = out_2[0].bitcast(I32)
        for q in range(4):
            queue = nc.sync if q < 2 else nc.scalar
            queue.dma_start(out_scales[4 * q : 4 * q + 4, :], y_scales[32 * q : 32 * q + 4, :].bitcast(I32))
